import numpy as np, ml_dtypes
CORES = [1,3,5,9,11,13]
N = 6
NB, TK, FT = 2, 64, 4
def setup_inputs(rng):
    return {"x": rng.standard_normal((N, NB, 128, TK), dtype=np.float32).astype(ml_dtypes.bfloat16), "w1": (rng.standard_normal((N, 128, FT * 128), dtype=np.float32) / 8).astype(ml_dtypes.bfloat16), "w2": (rng.standard_normal((N, 128, FT * 128), dtype=np.float32) / np.float32(8 * np.sqrt(FT))).astype(ml_dtypes.bfloat16)}
def setup_inputs_big(rng):
    d = setup_inputs(rng)
    for k in ("x",): d[k] = (d[k].astype(np.float32) * 1048576.0).astype(d[k].dtype)
    return d
def setup_inputs_small(rng):
    d = setup_inputs(rng)
    for k in ("x",): d[k] = (d[k].astype(np.float32) * (1 / 1048576.0)).astype(d[k].dtype)
    return d
def reference(x, w1, w2):
    W1, W2 = w1.astype(np.float64), w2.astype(np.float64)
    a = x[0].astype(np.float64)
    for s in range(N):
        a = sum(np.einsum("kf,bkn->bfn", W2[s][:, 128 * f:128 * f + 128], np.maximum(np.einsum("kf,bkn->bfn", W1[s][:, 128 * f:128 * f + 128], a), 0.0)) for f in range(FT))
    y = np.full(x.shape, np.nan, ml_dtypes.bfloat16)
    y[N - 1] = a.astype(ml_dtypes.bfloat16)
    return {"y": y}

@@ -1,0 +1,178 @@
+from concourse.mybir import AluOpType
+
+NB, TK, FT = 2, 64, 4
+P = 128
+GRP = 2
+GT = FT // GRP
+SLOTS = 3
+ACT_ENGINES = 8
+LOAD = 16
+
+MM, VE, HAND = 46, 67, 50
+LAG_LAST = 600
+LAG_SEND = 10 ** 6
+
+SCRATCH = {"zero": ("sbuf", [P, GT * TK], "float32")}
+SEMAPHORES = ["zs", "snt"]
+for _b in range(NB):
+    SCRATCH["ain%d" % _b] = ("sbuf", [P, TK], "bfloat16")
+    SCRATCH["acc%d" % _b] = ("psum", [P, 512], "float32")
+    SEMAPHORES += ["arr%d" % _b, "m2_%d" % _b, "cp%d" % _b, "st%d" % _b]
+    for _q in range(GRP):
+        SCRATCH["pre%d%d" % (_b, _q)] = ("psum", [P, 512], "float32")
+        SEMAPHORES += ["m1_%d%d" % (_b, _q), "rl%d%d" % (_b, _q)]
+    for _s in range(SLOTS):
+        SCRATCH["hid%d%d" % (_b, _s)] = ("sbuf", [P, FT * TK], "bfloat16")
+        SCRATCH["act%d%d" % (_b, _s)] = ("sbuf", [P, TK], "bfloat16")
+for _s in range(SLOTS):
+    SCRATCH["wt%d" % _s] = ("sbuf", [P, 2 * FT * P], "bfloat16")
+    SEMAPHORES += ["wa%d" % _s, "wb%d" % _s]
+
+
+def _plan(T, topo):
+    cores = list(T.cores)
+    first, last = cores[0], cores[-1]
+    gate = [c for c in cores if topo.chip(c) == topo.chip(first) and topo.may_write(c, last)][0]
+    site = []
+    for s, c in enumerate(cores):
+        if topo.chip(c) == topo.chip(last):
+            site.append(last)
+        elif s < cores.index(gate):
+            site.append(first)
+        else:
+            site.append(gate)
+    return site, [first, gate, last]
+
+
+def _engines(topo, src, dst, k):
+    m = topo.mask(src, dst)
+    bits = [i for i in range(m.bit_length()) if (m >> i) & 1][:k]
+    return sum(1 << i for i in bits), len(bits)
+
+
+def _order(nmaps, lag):
+    ops = {}
+    for b in range(NB):
+        for s in range(nmaps):
+            for q in range(GRP):
+                ops[("M1", b, s, q)] = ("T", GT * MM, [("C", b, s - 1, 0)] if s else [])
+                ops[("R", b, s, q)] = ("V", GT * VE, [("M1", b, s, q)])
+                ops[("M2", b, s, q)] = ("T", GT * MM, [("R", b, s, q)] + ([("M2", b, s, q - 1)] if q else []))
+            ops[("C", b, s, 0)] = ("V", VE, [("M2", b, s, GRP - 1)])
+    done, free, out = {}, {"T": 0, "V": 0}, []
+    while len(out) < len(ops):
+        best = None
+        for n, (e, d, deps) in ops.items():
+            if n in done or any(x not in done for x in deps):
+                continue
+            t = max([free[e], lag * n[1]] + [done[x] + (HAND if ops[x][0] != e else 0) for x in deps])
+            key = (t, n[1], n[2], n[3], n[0])
+            if best is None or key < best[0]:
+                best = (key, n)
+        n = best[1]
+        e, d, _ = ops[n]
+        done[n] = best[0][0] + d
+        free[e] = done[n]
+        out.append(n)
+    return out
+
+
+def _waiter(queue, T):
+    seen = {}
+
+    def wait(name, val):
+        if seen.get(name, 0) < val:
+            queue.wait_ge(T.sem[name], val)
+            seen[name] = val
+    return wait
+
+
+def rank_program(g, core, T, topo):
+    rank = T.rank_of(core)
+    if rank is None:
+        return
+    site, chain = _plan(T, topo)
+    cores = list(T.cores)
+    home = site[rank]
+    W = FT * P
+    halves = (("wa", 0, T.w1), ("wb", W, T.w2))
+
+    if home != core:
+        slot = [s for s in range(len(site)) if site[s] == home].index(rank)
+        mask, n = _engines(topo, core, home, LOAD)
+        rid, pid, _ = topo.addr(home)
+        for name, c0, src in halves:
+            g.sync.dma_start(T.wt0[:, c0:c0 + W], src[:, :]).then_inc(T.sem[name + "0"], LOAD)
+        for name, c0, src in halves:
+            g.wait_ge(T.sem[name + "0"], LOAD)
+            g.remote_dma(out_ap=T["wt%d" % slot][:, c0:c0 + W], in_ap=T.wt0[:, c0:c0 + W],
+                         remote_sem=T.sem["%s%d" % (name, slot)], local_sem=T.sem.snt,
+                         pid=pid, routing_id=rid, dma_engine_mask=mask)
+        g.wait_ge(T.sem.snt, 2 * n)
+        return
+
+    mine = [s for s in range(len(site)) if site[s] == core]
+    nmaps = len(mine)
+    pos = chain.index(core)
+    own = mine.index(rank)
+    wneed = [LOAD if s == rank else _engines(topo, cores[s], core, LOAD)[1] for s in mine]
+    wdst = T["wt%d" % own]
+    if pos == 0:
+        need_in = LOAD
+        g.sync.dma_start(T.ain0[:, :], T.x[0]).then_inc(T.sem.arr0, LOAD)
+        g.scalar.dma_start(wdst[:, 0:W], T.w1[:, :]).then_inc(T.sem["wa%d" % own], LOAD)
+        g.sync.dma_start(wdst[:, W:2 * W], T.w2[:, :]).then_inc(T.sem["wb%d" % own], LOAD)
+        g.sync.dma_start(T.ain1[:, :], T.x[1]).then_inc(T.sem.arr1, LOAD)
+    else:
+        need_in = _engines(topo, chain[pos - 1], core, ACT_ENGINES)[1]
+        g.sync.dma_start(wdst[:, 0:W], T.w1[:, :]).then_inc(T.sem["wa%d" % own], LOAD)
+        g.scalar.dma_start(wdst[:, W:2 * W], T.w2[:, :]).then_inc(T.sem["wb%d" % own], LOAD)
+
+    g.vector.memset(T.zero[:, :], 0.0).then_inc(T.sem.zs, 1)
+    tw, vw = _waiter(g.tensor, T), _waiter(g.vector, T)
+    is_last = pos == len(chain) - 1
+    for kind, b, s, q in _order(nmaps, LAG_LAST if is_last else LAG_SEND):
+        wt, hid, pre, acc = T["wt%d" % s], T["hid%d%d" % (b, s)], T["pre%d%d" % (b, q)], T["acc%d" % b]
+        if kind == "M1":
+            if s == 0:
+                tw("arr%d" % b, need_in)
+                a = T["ain%d" % b]
+            else:
+                tw("cp%d" % b, s)
+                a = T["act%d%d" % (b, s - 1)]
+            tw("wa%d" % s, wneed[s])
+            for j in range(GT):
+                f = q * GT + j
+                g.tensor.matmul(pre[:, j * TK:(j + 1) * TK], wt[:, f * P:(f + 1) * P], a[:, :],
+                                True, True).then_inc(T.sem["m1_%d%d" % (b, q)], 1)
+        elif kind == "R":
+            vw("zs", 1)
+            vw("m1_%d%d" % (b, q), GT * (s + 1))
+            g.vector.tensor_tensor(hid[:, q * GT * TK:(q + 1) * GT * TK], pre[:, 0:GT * TK], T.zero[:, :],
+                                   AluOpType.max).then_inc(T.sem["rl%d%d" % (b, q)], 1)
+        elif kind == "M2":
+            tw("rl%d%d" % (b, q), s + 1)
+            tw("wb%d" % s, wneed[s])
+            for j in range(GT):
+                f = q * GT + j
+                g.tensor.matmul(acc[:, 0:TK], wt[:, W + f * P:W + (f + 1) * P], hid[:, f * TK:(f + 1) * TK],
+                                f == 0, f == FT - 1).then_inc(T.sem["m2_%d" % b], 1)
+        else:
+            vw("m2_%d" % b, FT * (s + 1))
+            g.vector.tensor_copy(T["act%d%d" % (b, s)][:, :], acc[:, 0:TK]).then_inc(T.sem["cp%d" % b], 1)
+
+    if is_last:
+        for b, queue in enumerate((g.sync, g.scalar)):
+            queue.wait_ge(T.sem["cp%d" % b], nmaps)
+            queue.dma_start(T.y[b], T["act%d%d" % (b, nmaps - 1)][:, :]).then_inc(T.sem["st%d" % b], LOAD)
+            queue.wait_ge(T.sem["st%d" % b], LOAD)
+    else:
+        nxt = chain[pos + 1]
+        mask, n = _engines(topo, core, nxt, ACT_ENGINES)
+        rid, pid, _ = topo.addr(nxt)
+        for b in range(NB):
+            g.wait_ge(T.sem["cp%d" % b], nmaps)
+            g.remote_dma(out_ap=T["ain%d" % b][:, :], in_ap=T["act%d%d" % (b, nmaps - 1)][:, :],
+                         remote_sem=T.sem["arr%d" % b], local_sem=T.sem.snt,
+                         pid=pid, routing_id=rid, dma_engine_mask=mask)
+        g.wait_ge(T.sem.snt, NB * n)

@@ -8,8 +8,8 @@ SLOTS = 3
 ACT_ENGINES = 8
 LOAD = 16
 
-MM, VE, HAND = 46, 67, 50
-LAG_LAST = 600
+MM, VF, VE, HAND = 66, 70, 67, 45
+LAG_LAST = 950
 LAG_SEND = 10 ** 6
 
 SCRATCH = {"zero": ("sbuf", [P, GT * TK], "float32")}
@@ -41,7 +41,14 @@ def _plan(T, topo):
             site.append(first)
         else:
             site.append(gate)
-    return site, [first, gate, last]
+    where = [list(site) for _ in range(NB)]
+    for b in range(1, NB):
+        where[b][cores.index(gate)] = first
+    return where, [first, gate, last]
+
+
+def _maps_on(where, c):
+    return sorted({s for row in where for s in range(len(row)) if row[s] == c})
 
 
 def _engines(topo, src, dst, k):
@@ -50,15 +57,15 @@ def _engines(topo, src, dst, k):
     return sum(1 << i for i in bits), len(bits)
 
 
-def _order(nmaps, lag):
+def _order(nst, lag):
     ops = {}
     for b in range(NB):
-        for s in range(nmaps):
+        for s in range(nst[b]):
             for q in range(GRP):
                 ops[("M1", b, s, q)] = ("T", GT * MM, [("C", b, s - 1, 0)] if s else [])
-                ops[("R", b, s, q)] = ("V", GT * VE, [("M1", b, s, q)])
+                ops[("R", b, s, q)] = ("V", VF + GT * VE, [("M1", b, s, q)])
                 ops[("M2", b, s, q)] = ("T", GT * MM, [("R", b, s, q)] + ([("M2", b, s, q - 1)] if q else []))
-            ops[("C", b, s, 0)] = ("V", VE, [("M2", b, s, GRP - 1)])
+            ops[("C", b, s, 0)] = ("V", VF + VE, [("M2", b, s, GRP - 1)])
     done, free, out = {}, {"T": 0, "V": 0}, []
     while len(out) < len(ops):
         best = None
@@ -91,88 +98,91 @@ def rank_program(g, core, T, topo):
     rank = T.rank_of(core)
     if rank is None:
         return
-    site, chain = _plan(T, topo)
+    where, chain = _plan(T, topo)
     cores = list(T.cores)
-    home = site[rank]
     W = FT * P
-    halves = (("wa", 0, T.w1), ("wb", W, T.w2))
+    here = _maps_on(where, core)
+    own = here.index(rank) if rank in here else len(here)
+    wown = T["wt%d" % own]
+    others = sorted({row[rank] for row in where if row[rank] != core})
+    sent = 0
 
-    if home != core:
-        slot = [s for s in range(len(site)) if site[s] == home].index(rank)
-        mask, n = _engines(topo, core, home, LOAD)
-        rid, pid, _ = topo.addr(home)
-        for name, c0, src in halves:
-            g.sync.dma_start(T.wt0[:, c0:c0 + W], src[:, :]).then_inc(T.sem[name + "0"], LOAD)
-        for name, c0, src in halves:
-            g.wait_ge(T.sem[name + "0"], LOAD)
-            g.remote_dma(out_ap=T["wt%d" % slot][:, c0:c0 + W], in_ap=T.wt0[:, c0:c0 + W],
-                         remote_sem=T.sem["%s%d" % (name, slot)], local_sem=T.sem.snt,
-                         pid=pid, routing_id=rid, dma_engine_mask=mask)
-        g.wait_ge(T.sem.snt, 2 * n)
-        return
-
-    mine = [s for s in range(len(site)) if site[s] == core]
-    nmaps = len(mine)
-    pos = chain.index(core)
-    own = mine.index(rank)
-    wneed = [LOAD if s == rank else _engines(topo, cores[s], core, LOAD)[1] for s in mine]
-    wdst = T["wt%d" % own]
-    if pos == 0:
-        need_in = LOAD
+    if core == chain[0]:
         g.sync.dma_start(T.ain0[:, :], T.x[0]).then_inc(T.sem.arr0, LOAD)
-        g.scalar.dma_start(wdst[:, 0:W], T.w1[:, :]).then_inc(T.sem["wa%d" % own], LOAD)
-        g.sync.dma_start(wdst[:, W:2 * W], T.w2[:, :]).then_inc(T.sem["wb%d" % own], LOAD)
+        g.scalar.dma_start(wown[:, 0:W], T.w1[:, :]).then_inc(T.sem["wa%d" % own], LOAD)
+        g.sync.dma_start(wown[:, W:2 * W], T.w2[:, :]).then_inc(T.sem["wb%d" % own], LOAD)
         g.sync.dma_start(T.ain1[:, :], T.x[1]).then_inc(T.sem.arr1, LOAD)
     else:
-        need_in = _engines(topo, chain[pos - 1], core, ACT_ENGINES)[1]
-        g.sync.dma_start(wdst[:, 0:W], T.w1[:, :]).then_inc(T.sem["wa%d" % own], LOAD)
-        g.scalar.dma_start(wdst[:, W:2 * W], T.w2[:, :]).then_inc(T.sem["wb%d" % own], LOAD)
+        second = g.sync if others else g.scalar
+        g.sync.dma_start(wown[:, 0:W], T.w1[:, :]).then_inc(T.sem["wa%d" % own], LOAD)
+        second.dma_start(wown[:, W:2 * W], T.w2[:, :]).then_inc(T.sem["wb%d" % own], LOAD)
 
-    g.vector.memset(T.zero[:, :], 0.0).then_inc(T.sem.zs, 1)
-    tw, vw = _waiter(g.tensor, T), _waiter(g.vector, T)
-    is_last = pos == len(chain) - 1
-    for kind, b, s, q in _order(nmaps, LAG_LAST if is_last else LAG_SEND):
-        wt, hid, pre, acc = T["wt%d" % s], T["hid%d%d" % (b, s)], T["pre%d%d" % (b, q)], T["acc%d" % b]
-        if kind == "M1":
-            if s == 0:
-                tw("arr%d" % b, need_in)
-                a = T["ain%d" % b]
-            else:
-                tw("cp%d" % b, s)
-                a = T["act%d%d" % (b, s - 1)]
-            tw("wa%d" % s, wneed[s])
-            for j in range(GT):
-                f = q * GT + j
-                g.tensor.matmul(pre[:, j * TK:(j + 1) * TK], wt[:, f * P:(f + 1) * P], a[:, :],
-                                True, True).then_inc(T.sem["m1_%d%d" % (b, q)], 1)
-        elif kind == "R":
-            vw("zs", 1)
-            vw("m1_%d%d" % (b, q), GT * (s + 1))
-            g.vector.tensor_tensor(hid[:, q * GT * TK:(q + 1) * GT * TK], pre[:, 0:GT * TK], T.zero[:, :],
-                                   AluOpType.max).then_inc(T.sem["rl%d%d" % (b, q)], 1)
-        elif kind == "M2":
-            tw("rl%d%d" % (b, q), s + 1)
-            tw("wb%d" % s, wneed[s])
-            for j in range(GT):
-                f = q * GT + j
-                g.tensor.matmul(acc[:, 0:TK], wt[:, W + f * P:W + (f + 1) * P], hid[:, f * TK:(f + 1) * TK],
-                                f == 0, f == FT - 1).then_inc(T.sem["m2_%d" % b], 1)
-        else:
-            vw("m2_%d" % b, FT * (s + 1))
-            g.vector.tensor_copy(T["act%d%d" % (b, s)][:, :], acc[:, 0:TK]).then_inc(T.sem["cp%d" % b], 1)
-
-    if is_last:
-        for b, queue in enumerate((g.sync, g.scalar)):
-            queue.wait_ge(T.sem["cp%d" % b], nmaps)
-            queue.dma_start(T.y[b], T["act%d%d" % (b, nmaps - 1)][:, :]).then_inc(T.sem["st%d" % b], LOAD)
-            queue.wait_ge(T.sem["st%d" % b], LOAD)
-    else:
-        nxt = chain[pos + 1]
-        mask, n = _engines(topo, core, nxt, ACT_ENGINES)
-        rid, pid, _ = topo.addr(nxt)
-        for b in range(NB):
-            g.wait_ge(T.sem["cp%d" % b], nmaps)
-            g.remote_dma(out_ap=T["ain%d" % b][:, :], in_ap=T["act%d%d" % (b, nmaps - 1)][:, :],
-                         remote_sem=T.sem["arr%d" % b], local_sem=T.sem.snt,
+    for name, c0 in (("wa", 0), ("wb", W)):
+        for dst in others:
+            slot = _maps_on(where, dst).index(rank)
+            mask, n = _engines(topo, core, dst, LOAD)
+            rid, pid, _ = topo.addr(dst)
+            g.wait_ge(T.sem["%s%d" % (name, own)], LOAD)
+            g.remote_dma(out_ap=T["wt%d" % slot][:, c0:c0 + W], in_ap=wown[:, c0:c0 + W],
+                         remote_sem=T.sem["%s%d" % (name, slot)], local_sem=T.sem.snt,
                          pid=pid, routing_id=rid, dma_engine_mask=mask)
-        g.wait_ge(T.sem.snt, NB * n)
+            sent += n
+
+    if here:
+        pos = chain.index(core)
+        is_last = pos == len(chain) - 1
+        todo = [[here.index(s) for s in range(len(cores)) if where[b][s] == core] for b in range(NB)]
+        nst = [len(t) for t in todo]
+        wneed = [LOAD if s == rank else _engines(topo, cores[s], core, LOAD)[1] for s in here]
+        need_in = LOAD if pos == 0 else _engines(topo, chain[pos - 1], core, ACT_ENGINES)[1]
+
+        g.vector.memset(T.zero[:, :], 0.0).then_inc(T.sem.zs, 1)
+        tw, vw = _waiter(g.tensor, T), _waiter(g.vector, T)
+        for kind, b, s, q in _order(nst, LAG_LAST if is_last else LAG_SEND):
+            j = todo[b][s]
+            wt, hid, pre, acc = T["wt%d" % j], T["hid%d%d" % (b, s)], T["pre%d%d" % (b, q)], T["acc%d" % b]
+            if kind == "M1":
+                if s == 0:
+                    tw("arr%d" % b, need_in)
+                    a = T["ain%d" % b]
+                else:
+                    tw("cp%d" % b, s)
+                    a = T["act%d%d" % (b, s - 1)]
+                tw("wa%d" % j, wneed[j])
+                for i in range(GT):
+                    f = q * GT + i
+                    g.tensor.matmul(pre[:, i * TK:(i + 1) * TK], wt[:, f * P:(f + 1) * P], a[:, :],
+                                    True, True).then_inc(T.sem["m1_%d%d" % (b, q)], 1)
+            elif kind == "R":
+                vw("zs", 1)
+                vw("m1_%d%d" % (b, q), GT * (s + 1))
+                g.vector.tensor_tensor(hid[:, q * GT * TK:(q + 1) * GT * TK], pre[:, 0:GT * TK], T.zero[:, :],
+                                       AluOpType.max).then_inc(T.sem["rl%d%d" % (b, q)], 1)
+            elif kind == "M2":
+                tw("rl%d%d" % (b, q), s + 1)
+                tw("wb%d" % j, wneed[j])
+                for i in range(GT):
+                    f = q * GT + i
+                    g.tensor.matmul(acc[:, 0:TK], wt[:, W + f * P:W + (f + 1) * P], hid[:, f * TK:(f + 1) * TK],
+                                    f == 0, f == FT - 1).then_inc(T.sem["m2_%d" % b], 1)
+            else:
+                vw("m2_%d" % b, FT * (s + 1))
+                g.vector.tensor_copy(T["act%d%d" % (b, s)][:, :], acc[:, 0:TK]).then_inc(T.sem["cp%d" % b], 1)
+
+        if is_last:
+            for b, queue in enumerate((g.sync, g.scalar)):
+                queue.wait_ge(T.sem["cp%d" % b], nst[b])
+                queue.dma_start(T.y[b], T["act%d%d" % (b, nst[b] - 1)][:, :]).then_inc(T.sem["st%d" % b], LOAD)
+                queue.wait_ge(T.sem["st%d" % b], LOAD)
+        else:
+            nxt = chain[pos + 1]
+            mask, n = _engines(topo, core, nxt, ACT_ENGINES)
+            rid, pid, _ = topo.addr(nxt)
+            for b in range(NB):
+                g.wait_ge(T.sem["cp%d" % b], nst[b])
+                g.remote_dma(out_ap=T["ain%d" % b][:, :], in_ap=T["act%d%d" % (b, nst[b] - 1)][:, :],
+                             remote_sem=T.sem["arr%d" % b], local_sem=T.sem.snt,
+                             pid=pid, routing_id=rid, dma_engine_mask=mask)
+                sent += n
+    if sent:
+        g.wait_ge(T.sem.snt, sent)

@@ -9,7 +9,7 @@ ACT_ENGINES = 8
 LOAD = 16
 
 MM, VF, VE, HAND = 66, 70, 67, 45
-LAG_LAST = 950
+LAG_LAST = 800
 LAG_SEND = 10 ** 6
 
 SCRATCH = {"zero": ("sbuf", [P, GT * TK], "float32")}
@@ -57,7 +57,7 @@ def _engines(topo, src, dst, k):
     return sum(1 << i for i in bits), len(bits)
 
 
-def _order(nst, lag):
+def _order(nst, lag, late_first):
     ops = {}
     for b in range(NB):
         for s in range(nst[b]):
@@ -73,7 +73,7 @@ def _order(nst, lag):
             if n in done or any(x not in done for x in deps):
                 continue
             t = max([free[e], lag * n[1]] + [done[x] + (HAND if ops[x][0] != e else 0) for x in deps])
-            key = (t, n[1], n[2], n[3], n[0])
+            key = (t, -n[1] if late_first else n[1], n[2], n[3], n[0])
             if best is None or key < best[0]:
                 best = (key, n)
         n = best[1]
@@ -138,7 +138,7 @@ def rank_program(g, core, T, topo):
 
         g.vector.memset(T.zero[:, :], 0.0).then_inc(T.sem.zs, 1)
         tw, vw = _waiter(g.tensor, T), _waiter(g.vector, T)
-        for kind, b, s, q in _order(nst, LAG_LAST if is_last else LAG_SEND):
+        for kind, b, s, q in _order(nst, LAG_LAST if is_last else LAG_SEND, is_last):
             j = todo[b][s]
             wt, hid, pre, acc = T["wt%d" % j], T["hid%d%d" % (b, s)], T["pre%d%d" % (b, q)], T["acc%d" % b]
             if kind == "M1":

@@ -1,7 +1,9 @@
 from concourse.mybir import AluOpType
 
 NB, TK, FT = 2, 64, 4
+NCORES = 16
 P = 128
+W = FT * P
 GRP = 2
 GT = FT // GRP
 SLOTS = 3
@@ -9,8 +11,11 @@ ACT_ENGINES = 8
 LOAD = 16
 
 MM, VF, VE, HAND = 66, 70, 67, 45
-LAG_LAST = 800
-LAG_SEND = 10 ** 6
+LAG_FIRST = 10 ** 6
+LAG_LAST = 200
+
+WHOLE = (("wa", 0, W), ("wb", W, 2 * W))
+SPLIT = (("wc", 2 * W - GT * P, 2 * W), ("wa", 0, W), ("wb", W, 2 * W - GT * P))
 
 SCRATCH = {"zero": ("sbuf", [P, GT * TK], "float32")}
 SEMAPHORES = ["zs", "snt"]
@@ -25,30 +30,41 @@ for _b in range(NB):
         SCRATCH["hid%d%d" % (_b, _s)] = ("sbuf", [P, FT * TK], "bfloat16")
         SCRATCH["act%d%d" % (_b, _s)] = ("sbuf", [P, TK], "bfloat16")
 for _s in range(SLOTS):
-    SCRATCH["wt%d" % _s] = ("sbuf", [P, 2 * FT * P], "bfloat16")
-    SEMAPHORES += ["wa%d" % _s, "wb%d" % _s]
+    SCRATCH["wt%d" % _s] = ("sbuf", [P, 2 * W], "bfloat16")
+    SEMAPHORES += ["wa%d" % _s, "wb%d" % _s, "wc%d" % _s]
 
 
 def _plan(T, topo):
     cores = list(T.cores)
     first, last = cores[0], cores[-1]
-    gate = [c for c in cores if topo.chip(c) == topo.chip(first) and topo.may_write(c, last)][0]
-    site = []
-    for s, c in enumerate(cores):
-        if topo.chip(c) == topo.chip(last):
-            site.append(last)
-        elif s < cores.index(gate):
-            site.append(first)
-        else:
-            site.append(gate)
-    where = [list(site) for _ in range(NB)]
-    for b in range(1, NB):
-        where[b][cores.index(gate)] = first
-    return where, [first, gate, last]
+    gates = [c for c in range(NCORES) if topo.chip(c) == topo.chip(first) and topo.may_write(c, last)]
+    gate = [c for c in gates if c in cores][0]
+    free = [c for c in gates if c not in cores]
+    helper = ([c for c in free if topo.die(c) == topo.die(gate)] + free)[0]
+    where = []
+    for mid in (helper, gate):
+        where.append([last if topo.chip(c) == topo.chip(last) else first if s < cores.index(gate) else mid
+                      for s, c in enumerate(cores)])
+    return where, helper
 
 
 def _maps_on(where, c):
     return sorted({s for row in where for s in range(len(row)) if row[s] == c})
+
+
+def _routes(where, helper, cores):
+    pieces, routes = {}, []
+    for s, owner in enumerate(cores):
+        dsts = sorted({row[s] for row in where if row[s] != owner}, key=lambda d: (d != helper, d))
+        relay = helper in dsts and len(dsts) > 1
+        pieces[s] = SPLIT if relay else WHOLE
+        for k, piece in enumerate(pieces[s]):
+            if relay and k == 0:
+                routes.append((piece, s, owner, helper))
+                routes += [(piece, s, helper, d) for d in dsts if d != helper]
+            else:
+                routes += [(piece, s, owner, d) for d in dsts]
+    return pieces, routes
 
 
 def _engines(topo, src, dst, k):
@@ -96,59 +112,75 @@ def _waiter(queue, T):
 
 def rank_program(g, core, T, topo):
     rank = T.rank_of(core)
-    if rank is None:
+    where, helper = _plan(T, topo)
+    if rank is None and core != helper:
         return
-    where, chain = _plan(T, topo)
     cores = list(T.cores)
-    W = FT * P
+    first, last = cores[0], cores[-1]
+    pieces, routes = _routes(where, helper, cores)
     here = _maps_on(where, core)
-    own = here.index(rank) if rank in here else len(here)
-    wown = T["wt%d" % own]
-    others = sorted({row[rank] for row in where if row[rank] != core})
+    slot = {s: j for j, s in enumerate(here)}
+    if rank is not None and rank not in slot:
+        slot[rank] = len(here)
+    have = {}
+    for piece, s, src, dst in routes:
+        if dst == core:
+            have[(s, piece[0])] = _engines(topo, src, core, LOAD)[1]
     sent = 0
 
-    if core == chain[0]:
-        g.sync.dma_start(T.ain0[:, :], T.x[0]).then_inc(T.sem.arr0, LOAD)
-        g.scalar.dma_start(wown[:, 0:W], T.w1[:, :]).then_inc(T.sem["wa%d" % own], LOAD)
-        g.sync.dma_start(wown[:, W:2 * W], T.w2[:, :]).then_inc(T.sem["wb%d" % own], LOAD)
-        g.sync.dma_start(T.ain1[:, :], T.x[1]).then_inc(T.sem.arr1, LOAD)
-    else:
-        second = g.sync if others else g.scalar
-        g.sync.dma_start(wown[:, 0:W], T.w1[:, :]).then_inc(T.sem["wa%d" % own], LOAD)
-        second.dma_start(wown[:, W:2 * W], T.w2[:, :]).then_inc(T.sem["wb%d" % own], LOAD)
+    if rank is not None:
+        wown, own = T["wt%d" % slot[rank]], slot[rank]
+        sender = any(src == core for _, _, src, _ in routes)
+        if core == first:
+            g.sync.dma_start(T.ain0[:, :], T.x[0]).then_inc(T.sem.arr0, LOAD)
+        for k, (name, c0, c1) in enumerate(pieces[rank]):
+            queue = g.sync if sender or (k + (core == first)) % 2 == 0 else g.scalar
+            src = T.w1[:, c0:c1] if c1 <= W else T.w2[:, c0 - W:c1 - W]
+            queue.dma_start(wown[:, c0:c1], src).then_inc(T.sem["%s%d" % (name, own)], LOAD)
+            have[(rank, name)] = LOAD
+        if core == first:
+            g.sync.dma_start(T.ain1[:, :], T.x[1]).then_inc(T.sem.arr1, LOAD)
 
-    for name, c0 in (("wa", 0), ("wb", W)):
-        for dst in others:
-            slot = _maps_on(where, dst).index(rank)
-            mask, n = _engines(topo, core, dst, LOAD)
-            rid, pid, _ = topo.addr(dst)
-            g.wait_ge(T.sem["%s%d" % (name, own)], LOAD)
-            g.remote_dma(out_ap=T["wt%d" % slot][:, c0:c0 + W], in_ap=wown[:, c0:c0 + W],
-                         remote_sem=T.sem["%s%d" % (name, slot)], local_sem=T.sem.snt,
-                         pid=pid, routing_id=rid, dma_engine_mask=mask)
-            sent += n
+    for (name, c0, c1), s, src, dst in routes:
+        if src != core:
+            continue
+        there = _maps_on(where, dst).index(s)
+        mask, n = _engines(topo, core, dst, LOAD)
+        rid, pid, _ = topo.addr(dst)
+        g.wait_ge(T.sem["%s%d" % (name, slot[s])], have[(s, name)])
+        g.remote_dma(out_ap=T["wt%d" % there][:, c0:c1], in_ap=T["wt%d" % slot[s]][:, c0:c1],
+                     remote_sem=T.sem["%s%d" % (name, there)], local_sem=T.sem.snt,
+                     pid=pid, routing_id=rid, dma_engine_mask=mask)
+        sent += n
 
     if here:
-        pos = chain.index(core)
-        is_last = pos == len(chain) - 1
-        todo = [[here.index(s) for s in range(len(cores)) if where[b][s] == core] for b in range(NB)]
-        nst = [len(t) for t in todo]
-        wneed = [LOAD if s == rank else _engines(topo, cores[s], core, LOAD)[1] for s in here]
-        need_in = LOAD if pos == 0 else _engines(topo, chain[pos - 1], core, ACT_ENGINES)[1]
+        is_last = core == last
+        maps = [[s for s in range(len(cores)) if where[b][s] == core] for b in range(NB)]
+        nst = [len(m) for m in maps]
+        need_in = [0] * NB
+        for b in range(NB):
+            if nst[b]:
+                need_in[b] = LOAD if maps[b][0] == 0 else _engines(topo, where[b][maps[b][0] - 1], core, ACT_ENGINES)[1]
 
         g.vector.memset(T.zero[:, :], 0.0).then_inc(T.sem.zs, 1)
         tw, vw = _waiter(g.tensor, T), _waiter(g.vector, T)
-        for kind, b, s, q in _order(nst, LAG_LAST if is_last else LAG_SEND, is_last):
-            j = todo[b][s]
+        for kind, b, s, q in _order(nst, LAG_LAST if is_last else LAG_FIRST, is_last):
+            m = maps[b][s]
+            j = slot[m]
             wt, hid, pre, acc = T["wt%d" % j], T["hid%d%d" % (b, s)], T["pre%d%d" % (b, q)], T["acc%d" % b]
+            lo = (q * GT * P) + (W if kind == "M2" else 0)
+            hi = lo + GT * P
+            if kind in ("M1", "M2"):
+                for name, c0, c1 in pieces[m]:
+                    if c0 < hi and lo < c1:
+                        tw("%s%d" % (name, j), have[(m, name)])
             if kind == "M1":
                 if s == 0:
-                    tw("arr%d" % b, need_in)
+                    tw("arr%d" % b, need_in[b])
                     a = T["ain%d" % b]
                 else:
                     tw("cp%d" % b, s)
                     a = T["act%d%d" % (b, s - 1)]
-                tw("wa%d" % j, wneed[j])
                 for i in range(GT):
                     f = q * GT + i
                     g.tensor.matmul(pre[:, i * TK:(i + 1) * TK], wt[:, f * P:(f + 1) * P], a[:, :],
@@ -160,7 +192,6 @@ def rank_program(g, core, T, topo):
                                        AluOpType.max).then_inc(T.sem["rl%d%d" % (b, q)], 1)
             elif kind == "M2":
                 tw("rl%d%d" % (b, q), s + 1)
-                tw("wb%d" % j, wneed[j])
                 for i in range(GT):
                     f = q * GT + i
                     g.tensor.matmul(acc[:, 0:TK], wt[:, W + f * P:W + (f + 1) * P], hid[:, f * TK:(f + 1) * TK],
@@ -175,10 +206,12 @@ def rank_program(g, core, T, topo):
                 queue.dma_start(T.y[b], T["act%d%d" % (b, nst[b] - 1)][:, :]).then_inc(T.sem["st%d" % b], LOAD)
                 queue.wait_ge(T.sem["st%d" % b], LOAD)
         else:
-            nxt = chain[pos + 1]
-            mask, n = _engines(topo, core, nxt, ACT_ENGINES)
-            rid, pid, _ = topo.addr(nxt)
             for b in range(NB):
+                if not nst[b]:
+                    continue
+                nxt = where[b][maps[b][-1] + 1]
+                mask, n = _engines(topo, core, nxt, ACT_ENGINES)
+                rid, pid, _ = topo.addr(nxt)
                 g.wait_ge(T.sem["cp%d" % b], nst[b])
                 g.remote_dma(out_ap=T["ain%d" % b][:, :], in_ap=T["act%d%d" % (b, nst[b] - 1)][:, :],
                              remote_sem=T.sem["arr%d" % b], local_sem=T.sem.snt,

from concourse.mybir import AluOpType

NB, TK, FT = 2, 64, 4
NCORES = 16
P = 128
W = FT * P
GRP = 2
GT = FT // GRP
SLOTS = 3
ACT_ENGINES = 8
LOAD = 16

MM, VF, VE, HAND = 66, 70, 67, 45
LAG_FIRST = 10 ** 6
LAG_LAST = 200

WHOLE = (("wa", 0, W), ("wb", W, 2 * W))
SPLIT = (("wc", 2 * W - GT * P, 2 * W), ("wa", 0, W), ("wb", W, 2 * W - GT * P))

SCRATCH = {"zero": ("sbuf", [P, GT * TK], "float32")}
SEMAPHORES = ["zs", "snt"]
for _b in range(NB):
    SCRATCH["ain%d" % _b] = ("sbuf", [P, TK], "bfloat16")
    SCRATCH["acc%d" % _b] = ("psum", [P, 512], "float32")
    SEMAPHORES += ["arr%d" % _b, "m2_%d" % _b, "cp%d" % _b, "st%d" % _b]
    for _q in range(GRP):
        SCRATCH["pre%d%d" % (_b, _q)] = ("psum", [P, 512], "float32")
        SEMAPHORES += ["m1_%d%d" % (_b, _q), "rl%d%d" % (_b, _q)]
    for _s in range(SLOTS):
        SCRATCH["hid%d%d" % (_b, _s)] = ("sbuf", [P, FT * TK], "bfloat16")
        SCRATCH["act%d%d" % (_b, _s)] = ("sbuf", [P, TK], "bfloat16")
for _s in range(SLOTS):
    SCRATCH["wt%d" % _s] = ("sbuf", [P, 2 * W], "bfloat16")
    SEMAPHORES += ["wa%d" % _s, "wb%d" % _s, "wc%d" % _s]


def _plan(T, topo):
    cores = list(T.cores)
    first, last = cores[0], cores[-1]
    gates = [c for c in range(NCORES) if topo.chip(c) == topo.chip(first) and topo.may_write(c, last)]
    gate = [c for c in gates if c in cores][0]
    free = [c for c in gates if c not in cores]
    helper = ([c for c in free if topo.die(c) == topo.die(gate)] + free)[0]
    where = []
    for mid in (helper, gate):
        where.append([last if topo.chip(c) == topo.chip(last) else first if s < cores.index(gate) else mid
                      for s, c in enumerate(cores)])
    return where, helper


def _maps_on(where, c):
    return sorted({s for row in where for s in range(len(row)) if row[s] == c})


def _routes(where, helper, cores):
    pieces, routes = {}, []
    for s, owner in enumerate(cores):
        dsts = sorted({row[s] for row in where if row[s] != owner}, key=lambda d: (d != helper, d))
        relay = helper in dsts and len(dsts) > 1
        pieces[s] = SPLIT if relay else WHOLE
        for k, piece in enumerate(pieces[s]):
            if relay and k == 0:
                routes.append((piece, s, owner, helper))
                routes += [(piece, s, helper, d) for d in dsts if d != helper]
            else:
                routes += [(piece, s, owner, d) for d in dsts]
    return pieces, routes


def _engines(topo, src, dst, k):
    m = topo.mask(src, dst)
    bits = [i for i in range(m.bit_length()) if (m >> i) & 1][:k]
    return sum(1 << i for i in bits), len(bits)


def _order(nst, lag, late_first):
    ops = {}
    for b in range(NB):
        for s in range(nst[b]):
            for q in range(GRP):
                ops[("M1", b, s, q)] = ("T", GT * MM, [("C", b, s - 1, 0)] if s else [])
                ops[("R", b, s, q)] = ("V", VF + GT * VE, [("M1", b, s, q)])
                ops[("M2", b, s, q)] = ("T", GT * MM, [("R", b, s, q)] + ([("M2", b, s, q - 1)] if q else []))
            ops[("C", b, s, 0)] = ("V", VF + VE, [("M2", b, s, GRP - 1)])
    done, free, out = {}, {"T": 0, "V": 0}, []
    while len(out) < len(ops):
        best = None
        for n, (e, d, deps) in ops.items():
            if n in done or any(x not in done for x in deps):
                continue
            t = max([free[e], lag * n[1]] + [done[x] + (HAND if ops[x][0] != e else 0) for x in deps])
            key = (t, -n[1] if late_first else n[1], n[2], n[3], n[0])
            if best is None or key < best[0]:
                best = (key, n)
        n = best[1]
        e, d, _ = ops[n]
        done[n] = best[0][0] + d
        free[e] = done[n]
        out.append(n)
    return out


def _waiter(queue, T):
    seen = {}

    def wait(name, val):
        if seen.get(name, 0) < val:
            queue.wait_ge(T.sem[name], val)
            seen[name] = val
    return wait


def rank_program(g, core, T, topo):
    rank = T.rank_of(core)
    where, helper = _plan(T, topo)
    if rank is None and core != helper:
        return
    cores = list(T.cores)
    first, last = cores[0], cores[-1]
    pieces, routes = _routes(where, helper, cores)
    here = _maps_on(where, core)
    slot = {s: j for j, s in enumerate(here)}
    if rank is not None and rank not in slot:
        slot[rank] = len(here)
    have = {}
    for piece, s, src, dst in routes:
        if dst == core:
            have[(s, piece[0])] = _engines(topo, src, core, LOAD)[1]
    sent = 0

    if rank is not None:
        wown, own = T["wt%d" % slot[rank]], slot[rank]
        sender = any(src == core for _, _, src, _ in routes)
        if core == first:
            g.sync.dma_start(T.ain0[:, :], T.x[0]).then_inc(T.sem.arr0, LOAD)
        for k, (name, c0, c1) in enumerate(pieces[rank]):
            queue = g.sync if sender or (k + (core == first)) % 2 == 0 else g.scalar
            src = T.w1[:, c0:c1] if c1 <= W else T.w2[:, c0 - W:c1 - W]
            queue.dma_start(wown[:, c0:c1], src).then_inc(T.sem["%s%d" % (name, own)], LOAD)
            have[(rank, name)] = LOAD
        if core == first:
            g.sync.dma_start(T.ain1[:, :], T.x[1]).then_inc(T.sem.arr1, LOAD)

    for (name, c0, c1), s, src, dst in routes:
        if src != core:
            continue
        there = _maps_on(where, dst).index(s)
        mask, n = _engines(topo, core, dst, LOAD)
        rid, pid, _ = topo.addr(dst)
        g.wait_ge(T.sem["%s%d" % (name, slot[s])], have[(s, name)])
        g.remote_dma(out_ap=T["wt%d" % there][:, c0:c1], in_ap=T["wt%d" % slot[s]][:, c0:c1],
                     remote_sem=T.sem["%s%d" % (name, there)], local_sem=T.sem.snt,
                     pid=pid, routing_id=rid, dma_engine_mask=mask)
        sent += n

    if here:
        is_last = core == last
        maps = [[s for s in range(len(cores)) if where[b][s] == core] for b in range(NB)]
        nst = [len(m) for m in maps]
        need_in = [0] * NB
        for b in range(NB):
            if nst[b]:
                need_in[b] = LOAD if maps[b][0] == 0 else _engines(topo, where[b][maps[b][0] - 1], core, ACT_ENGINES)[1]

        g.vector.memset(T.zero[:, :], 0.0).then_inc(T.sem.zs, 1)
        tw, vw = _waiter(g.tensor, T), _waiter(g.vector, T)
        for kind, b, s, q in _order(nst, LAG_LAST if is_last else LAG_FIRST, is_last):
            m = maps[b][s]
            j = slot[m]
            wt, hid, pre, acc = T["wt%d" % j], T["hid%d%d" % (b, s)], T["pre%d%d" % (b, q)], T["acc%d" % b]
            lo = (q * GT * P) + (W if kind == "M2" else 0)
            hi = lo + GT * P
            if kind in ("M1", "M2"):
                for name, c0, c1 in pieces[m]:
                    if c0 < hi and lo < c1:
                        tw("%s%d" % (name, j), have[(m, name)])
            if kind == "M1":
                if s == 0:
                    tw("arr%d" % b, need_in[b])
                    a = T["ain%d" % b]
                else:
                    tw("cp%d" % b, s)
                    a = T["act%d%d" % (b, s - 1)]
                for i in range(GT):
                    f = q * GT + i
                    g.tensor.matmul(pre[:, i * TK:(i + 1) * TK], wt[:, f * P:(f + 1) * P], a[:, :],
                                    True, True).then_inc(T.sem["m1_%d%d" % (b, q)], 1)
            elif kind == "R":
                vw("zs", 1)
                vw("m1_%d%d" % (b, q), GT * (s + 1))
                g.vector.tensor_tensor(hid[:, q * GT * TK:(q + 1) * GT * TK], pre[:, 0:GT * TK], T.zero[:, :],
                                       AluOpType.max).then_inc(T.sem["rl%d%d" % (b, q)], 1)
            elif kind == "M2":
                tw("rl%d%d" % (b, q), s + 1)
                for i in range(GT):
                    f = q * GT + i
                    g.tensor.matmul(acc[:, 0:TK], wt[:, W + f * P:W + (f + 1) * P], hid[:, f * TK:(f + 1) * TK],
                                    f == 0, f == FT - 1).then_inc(T.sem["m2_%d" % b], 1)
            else:
                vw("m2_%d" % b, FT * (s + 1))
                g.vector.tensor_copy(T["act%d%d" % (b, s)][:, :], acc[:, 0:TK]).then_inc(T.sem["cp%d" % b], 1)

        if is_last:
            for b, queue in enumerate((g.sync, g.scalar)):
                queue.wait_ge(T.sem["cp%d" % b], nst[b])
                queue.dma_start(T.y[b], T["act%d%d" % (b, nst[b] - 1)][:, :]).then_inc(T.sem["st%d" % b], LOAD)
                queue.wait_ge(T.sem["st%d" % b], LOAD)
        else:
            for b in range(NB):
                if not nst[b]:
                    continue
                nxt = where[b][maps[b][-1] + 1]
                mask, n = _engines(topo, core, nxt, ACT_ENGINES)
                rid, pid, _ = topo.addr(nxt)
                g.wait_ge(T.sem["cp%d" % b], nst[b])
                g.remote_dma(out_ap=T["ain%d" % b][:, :], in_ap=T["act%d%d" % (b, nst[b] - 1)][:, :],
                             remote_sem=T.sem["arr%d" % b], local_sem=T.sem.snt,
                             pid=pid, routing_id=rid, dma_engine_mask=mask)
                sent += n
    if sent:
        g.wait_ge(T.sem.snt, sent)
